import numpy as np, ml_dtypes
CORES = [9,25,41,57]
N = 4
import mx_ref
BF = ml_dtypes.bfloat16
def gentries(a):
    return np.ascontiguousarray(a.reshape(8, 16, -1).transpose(0, 2, 1)).reshape(8, -1)
def gtable(e):
    e = np.asarray(e); return np.ascontiguousarray(e.reshape(8, -1, 16).transpose(0, 2, 1)).reshape(128, -1).astype(np.int32)
def gcols(t, e):
    v = np.concatenate([t.reshape(8, 16, -1, 4), np.zeros((8, 16, 1, 4), BF)], axis=2)
    return np.ascontiguousarray(np.stack([v[g][:, e[g]] for g in range(8)])).reshape(128, -1)
def f(rng, *shape):
    return mx_ref.flush((rng.standard_normal(shape, dtype=np.float32) * np.exp2(rng.integers(-2, 3, shape[:-1] + (1,)))).astype(BF))
def wide(rng, *shape, cols=0):
    v = rng.standard_normal(shape, dtype=np.float32) * np.exp2(rng.integers(-12, 13, shape)).astype(np.float32)
    if cols: v *= np.repeat(np.exp2(rng.integers(-cols, cols + 1, shape[:-2] + (1, shape[-1] // 4))) * (rng.random(shape[:-2] + (1, shape[-1] // 4)) > 0.0625), 4, axis=-1).astype(np.float32)
    return mx_ref.flush(v.astype(BF))
S = 512
def block(rng, how):
    if how == "one": return np.full((8, S), rng.integers(0, 128))
    if how == "groups": return np.tile(rng.integers(0, 128, S), (8, 1))
    if how == "ends": return np.stack([rng.permutation(np.arange(S) % 2 * 127) for g in range(8)])
    if how == "distinct": return np.stack([np.tile(rng.permutation(128), S // 128) for g in range(8)])
    return rng.integers(0, 128, (8, S))
def lists(rng, how=""):
    return {"cw": np.stack([gtable(np.concatenate([block(rng, how) for s in range(N)], axis=1)) for r in range(N)])}
def setup_inputs(rng):
    return {"bk": f(rng, N, 128, 512), "x": f(rng, N, 128, 512 * N), **lists(rng)}
def setup_inputs_one(rng):
    return {**setup_inputs(rng), **lists(rng, "one")}
def setup_inputs_groups(rng):
    return {**setup_inputs(rng), **lists(rng, "groups")}
def setup_inputs_ends(rng):
    return {**setup_inputs(rng), **lists(rng, "ends")}
def setup_inputs_distinct(rng):
    return {**setup_inputs(rng), **lists(rng, "distinct")}
def setup_inputs_spread(rng):
    d = setup_inputs(rng); d["bk"] = wide(rng, N, 128, 512, cols=4); d["x"] = wide(rng, N, 128, 512 * N); return d
def check_inputs(d):
    b = []
    for r in range(N):
        e = d["cw"][r]
        if e.min() < 0 or e.max() > 127: b.append("cw")
    return b
def reference(bk, x, cw):
    y = np.zeros((N, 128, S), np.float32)
    for r in range(N):
        e = gentries(cw[r])
        for s in range(N):
            W = gcols(bk[s], e[:, S * s:S * s + S])
            X = np.ascontiguousarray(x[r][:, 512 * s:512 * s + 512])
            y[r] += mx_ref.matmul(mx_ref.quantize(X), mx_ref.quantize(W))
    return {"y": y}

@@ -1,0 +1,138 @@
+from concourse.mybir import dt, ActivationFunctionType
+
+N = 4
+S = 512
+CODES = "float8_e4m3fn_x4"
+SPLIT = 320
+LIST_ENGINES = 4
+
+SCRATCH = {
+    "cwi": ("sbuf", [128, 128], "int32"),
+    "lst": ("sbuf", [128, 128], "uint16"),
+    "bks": ("sbuf", [128, 512], "bfloat16"),
+    "bd": ("sbuf", [128, 512], "bfloat16"),
+    "xs": ("sbuf", [128, 2048], "bfloat16"),
+    "xq": ("sbuf", [128, 512], CODES),
+    "xp": ("sbuf", [128, 512], "uint8"),
+    "yo": ("sbuf", [128, 512], "float32"),
+    "ps": ("psum", [128, 1024], "float32"),
+}
+SEMAPHORES = ["cw_in", "bk_in", "x_in", "lst_v", "lst_s", "bd_v", "bd_s", "bd_1", "x_q", "sent", "mm_a", "mm_b", "y_v", "y_s", "out_a", "out_b"]
+for _k in range(N):
+    SCRATCH["w%d" % _k] = ("sbuf", [128, 4 * S], "bfloat16")
+    SCRATCH["wq%d" % _k] = ("sbuf", [128, S], CODES)
+    SCRATCH["wp%d" % _k] = ("sbuf", [128, S], "uint8")
+    SEMAPHORES += ["gv%d" % _k, "gs%d" % _k, "q%d" % _k]
+    if _k:
+        SCRATCH["la%d" % _k] = ("sbuf", [128, 32], "uint16")
+        SCRATCH["aq%d" % _k] = ("sbuf", [128, S], CODES)
+        SCRATCH["ap%d" % _k] = ("sbuf", [128, S], "uint8")
+        SEMAPHORES += ["la%d" % _k, "lb%d" % _k, "arr%d" % _k]
+
+
+def mask_of(engines):
+    return sum(1 << e for e in engines)
+
+
+def rank_program(g, core, T, topo):
+    rank = T.rank_of(core)
+    if rank is None:
+        return
+    cores = T.cores
+    sem = T.sem
+    copy = ActivationFunctionType.Copy
+
+    def send(dst, out, in_, remote_sem, engines):
+        rid, pid, _ = topo.addr(dst)
+        g.remote_dma(out, in_, remote_sem, sem.sent, pid, rid, mask_of(engines))
+        return len(engines)
+
+    g.sync.dma_start(T.cwi[:], T.cw[:]).then_inc(sem.cw_in, 16)
+    g.scalar.dma_start(T.bks[:], T.bk[:]).then_inc(sem.bk_in, 16)
+    g.sync.dma_start(T.xs[:], T.x[:]).then_inc(sem.x_in, 16)
+
+    g.vector.wait_ge(sem.cw_in, 16)
+    g.vector.tensor_copy(T.lst[:], T.cwi[:]).then_inc(sem.lst_v, 1)
+    g.vector.wait_ge(sem.bk_in, 16)
+    for t in (0, 1):
+        g.vector.tensor_copy(T.bd[:, 128 * t:128 * t + 128], T.bks[:, t:512:4]).then_inc(sem.bd_v, 1)
+    g.scalar.wait_ge(sem.bk_in, 16)
+    for t in (2, 3):
+        g.scalar.activation(T.bd[:, 128 * t:128 * t + 128], T.bks[:, t:512:4], copy).then_inc(sem.bd_s, 1)
+    g.vector.wait_ge(sem.bd_v, 2)
+    g.scalar.wait_ge(sem.bd_s, 2)
+    g.scalar.wait_ge(sem.bd_v, 2)
+
+    sent = 0
+    g.wait_ge(sem.lst_v, 1)
+    for k in range(1, N):
+        s = (rank - k) % N
+        dst = cores[s]
+        sent += send(dst, T["la%d" % k][:], T.lst[:, 32 * s:32 * s + 32], sem["la%d" % k], topo.engines(core, dst)[:LIST_ENGINES])
+
+    g.vector.wait_ge(sem.lst_v, 1)
+    g.scalar.wait_ge(sem.lst_v, 1)
+    for k in range(N):
+        r = (rank + k) % N
+        w = T["w%d" % k]
+        if k == 0:
+            off, o0 = T.lst, 32 * rank
+        else:
+            off, o0 = T["la%d" % k], 0
+            need = len(topo.engines(cores[r], core)[:LIST_ENGINES])
+            g.vector.wait_ge(sem["la%d" % k], need)
+            g.scalar.wait_ge(sem["la%d" % k], need)
+
+        def gather(queue, t, a, b, done):
+            out = w[:, 4 * a + t:4 * b:4]
+            in_ = T.bd[:, 128 * t:128 * t + 128].indirect(off[:, o0 + a // 16:o0 + b // 16])
+            if queue == "v":
+                g.vector.tensor_copy(out, in_).then_inc(done, 1)
+            else:
+                g.scalar.activation(out, in_, copy).then_inc(done, 1)
+
+        gather("v", 0, 0, S, sem["gv%d" % k])
+        gather("v", 1, 0, SPLIT, sem["gv%d" % k])
+        gather("s", 2, 0, S, sem["gs%d" % k])
+        gather("s", 3, 0, S, sem["gs%d" % k])
+        gather("s", 1, SPLIT, S, sem["gs%d" % k])
+        if k == 0:
+            g.vector.wait_ge(sem.x_in, 16)
+            g.vector.quantize_mx(T.xq[:], T.xp[:], T.xs[:]).then_inc(sem.x_q, 1)
+        g.vector.wait_ge(sem["gv%d" % k], 2)
+        g.vector.wait_ge(sem["gs%d" % k], 3)
+        g.vector.quantize_mx(T["wq%d" % k][:], T["wp%d" % k][:], w[:]).then_inc(sem["q%d" % k], 1)
+
+        if k:
+            dst = cores[r]
+            eng = topo.engines(core, dst)
+            g.wait_ge(sem["q%d" % k], 1)
+            sent += send(dst, T["aq%d" % k][:].bitcast(dt.uint8), T["wq%d" % k][:].bitcast(dt.uint8), sem["arr%d" % k], eng)
+            sent += send(dst, T["ap%d" % k][:], T["wp%d" % k][:], sem["arr%d" % k], eng)
+
+    g.tensor.wait_ge(sem.x_q, 1)
+    for k in range(N):
+        s = (rank - k) % N
+        if k == 0:
+            g.tensor.wait_ge(sem.q0, 1)
+            q, p = T.wq0, T.wp0
+        else:
+            g.tensor.wait_ge(sem["arr%d" % k], 2 * len(topo.engines(cores[s], core)))
+            q, p = T["aq%d" % k], T["ap%d" % k]
+        for h, done in ((0, sem.mm_a), (1, sem.mm_b)):
+            m = g.tensor.matmul_mx(T.ps[:, 512 * h:512 * h + 256], T.xq[:, 128 * s:128 * s + 128], T.xp[:, 128 * s:128 * s + 128],
+                                   q[:, 256 * h:256 * h + 256], p[:, 256 * h:256 * h + 256], k == 0, k == N - 1)
+            if k == N - 1:
+                m.then_inc(done, 1)
+
+    g.vector.wait_ge(sem.mm_a, 1)
+    g.vector.tensor_copy(T.yo[:, 0:256], T.ps[:, 0:256]).then_inc(sem.y_v, 1)
+    g.sync.wait_ge(sem.y_v, 1)
+    g.sync.dma_start(T.y[:, 0:256], T.yo[:, 0:256]).then_inc(sem.out_a, 16)
+    g.sync.wait_ge(sem.out_a, 16)
+    g.scalar.wait_ge(sem.mm_b, 1)
+    g.scalar.activation(T.yo[:, 256:512], T.ps[:, 512:768], copy).then_inc(sem.y_s, 1)
+    g.scalar.wait_ge(sem.y_s, 1)
+    g.scalar.dma_start(T.y[:, 256:512], T.yo[:, 256:512]).then_inc(sem.out_b, 16)
+    g.scalar.wait_ge(sem.out_b, 16)
+    g.wait_ge(sem.sent, sent)

@@ -1,10 +1,20 @@
+from concourse.bass import DstId, RemoteDMATransfer
 from concourse.mybir import dt, ActivationFunctionType
 
 N = 4
 S = 512
+H = S // 2
 CODES = "float8_e4m3fn_x4"
-SPLIT = 320
 LIST_ENGINES = 4
+ORDER = [
+    (0, 0, H, (256, 160, 0, 0), "own"),
+    (1, 0, H, (256, 192, 0, 0), "helper"),
+    (1, H, S, (256, 192, 0, 0), "direct"),
+    (2, 0, S, (512, 384, 0, 0), "both"),
+    (3, 0, H, (256, 192, 0, 0), "helper"),
+    (3, H, S, (256, 192, 0, 0), "direct"),
+    (0, H, S, (256, 192, 0, 0), "own"),
+]
 
 SCRATCH = {
     "cwi": ("sbuf", [128, 128], "int32"),
@@ -17,35 +27,69 @@ SCRATCH = {
     "yo": ("sbuf", [128, 512], "float32"),
     "ps": ("psum", [128, 1024], "float32"),
 }
-SEMAPHORES = ["cw_in", "bk_in", "x_in", "lst_v", "lst_s", "bd_v", "bd_s", "bd_1", "x_q", "sent", "mm_a", "mm_b", "y_v", "y_s", "out_a", "out_b"]
+SEMAPHORES = ["cw_in", "bk_in", "x_in", "lst_v", "bd_v", "bd_s", "x_q", "sent", "mm_a", "mm_b", "y_v", "y_s", "out_a", "out_b"]
+for _i in range(len(ORDER)):
+    SEMAPHORES += ["gv%d" % _i, "gs%d" % _i, "q%d" % _i, "hop%d" % _i]
 for _k in range(N):
     SCRATCH["w%d" % _k] = ("sbuf", [128, 4 * S], "bfloat16")
     SCRATCH["wq%d" % _k] = ("sbuf", [128, S], CODES)
     SCRATCH["wp%d" % _k] = ("sbuf", [128, S], "uint8")
-    SEMAPHORES += ["gv%d" % _k, "gs%d" % _k, "q%d" % _k]
     if _k:
         SCRATCH["la%d" % _k] = ("sbuf", [128, 32], "uint16")
         SCRATCH["aq%d" % _k] = ("sbuf", [128, S], CODES)
         SCRATCH["ap%d" % _k] = ("sbuf", [128, S], "uint8")
-        SEMAPHORES += ["la%d" % _k, "lb%d" % _k, "arr%d" % _k]
+        SEMAPHORES += ["la%d" % _k, "arr%d" % _k]
 
 
 def mask_of(engines):
     return sum(1 << e for e in engines)
 
 
+def helper_of(core, dsts, topo):
+    return [h for h in topo.cores_of(core) if topo.die(h) != topo.die(core) and all(topo.may_write(h, d) for d in dsts)][0]
+
+
+def hop_engines(src, helper, dst, topo):
+    off = topo.engines(src, dst)
+    return [e for e in topo.engines(src, helper) if e not in off]
+
+
+def handed_on(a, b, roads):
+    return {"helper": (a, b), "both": (a, (a + b) // 2)}[roads]
+
+
 def rank_program(g, core, T, topo):
-    rank = T.rank_of(core)
-    if rank is None:
-        return
     cores = T.cores
     sem = T.sem
     copy = ActivationFunctionType.Copy
+
+    def codes(name, k, a, b):
+        return T["%s%d" % (name, k)][:, a:b].bitcast(dt.uint8)
 
     def send(dst, out, in_, remote_sem, engines):
         rid, pid, _ = topo.addr(dst)
         g.remote_dma(out, in_, remote_sem, sem.sent, pid, rid, mask_of(engines))
         return len(engines)
+
+    def transfer(dst, out, in_, remote_sem, engines):
+        rid, pid, _ = topo.addr(dst)
+        return RemoteDMATransfer(dst_ids=[DstId(rid=rid, pnc=pid)], dma_engine_mask=mask_of(engines), remote_sem=remote_sem, src=in_, dst=out)
+
+    helpers = [helper_of(cores[r], [c for c in cores if c != cores[r]], topo) for r in range(N)]
+    rank = T.rank_of(core)
+    if rank is None:
+        if core not in helpers:
+            return
+        r = helpers.index(core)
+        sent = 0
+        for i, (k, a, b, share, roads) in enumerate(ORDER):
+            if roads in ("helper", "both"):
+                a, b = handed_on(a, b, roads)
+                dst = cores[(r + k) % N]
+                g.wait_ge(sem["hop%d" % i], len(hop_engines(cores[r], core, dst, topo)))
+                sent += send(dst, codes("aq", k, a, b), codes("aq", k, a, b), sem["arr%d" % k], topo.engines(core, dst))
+        g.wait_ge(sem.sent, sent)
+        return
 
     g.sync.dma_start(T.cwi[:], T.cw[:]).then_inc(sem.cw_in, 16)
     g.scalar.dma_start(T.bks[:], T.bk[:]).then_inc(sem.bk_in, 16)
@@ -59,9 +103,10 @@ def rank_program(g, core, T, topo):
     g.scalar.wait_ge(sem.bk_in, 16)
     for t in (2, 3):
         g.scalar.activation(T.bd[:, 128 * t:128 * t + 128], T.bks[:, t:512:4], copy).then_inc(sem.bd_s, 1)
-    g.vector.wait_ge(sem.bd_v, 2)
-    g.scalar.wait_ge(sem.bd_s, 2)
-    g.scalar.wait_ge(sem.bd_v, 2)
+    for q in (g.vector, g.scalar):
+        q.wait_ge(sem.bd_v, 2)
+        q.wait_ge(sem.bd_s, 2)
+        q.wait_ge(sem.lst_v, 1)
 
     sent = 0
     g.wait_ge(sem.lst_v, 1)
@@ -70,69 +115,89 @@ def rank_program(g, core, T, topo):
         dst = cores[s]
         sent += send(dst, T["la%d" % k][:], T.lst[:, 32 * s:32 * s + 32], sem["la%d" % k], topo.engines(core, dst)[:LIST_ENGINES])
 
-    g.vector.wait_ge(sem.lst_v, 1)
-    g.scalar.wait_ge(sem.lst_v, 1)
-    for k in range(N):
+    for i, (k, a, b, share, roads) in enumerate(ORDER):
         r = (rank + k) % N
         w = T["w%d" % k]
         if k == 0:
             off, o0 = T.lst, 32 * rank
         else:
             off, o0 = T["la%d" % k], 0
-            need = len(topo.engines(cores[r], core)[:LIST_ENGINES])
-            g.vector.wait_ge(sem["la%d" % k], need)
-            g.scalar.wait_ge(sem["la%d" % k], need)
-
-        def gather(queue, t, a, b, done):
-            out = w[:, 4 * a + t:4 * b:4]
-            in_ = T.bd[:, 128 * t:128 * t + 128].indirect(off[:, o0 + a // 16:o0 + b // 16])
-            if queue == "v":
-                g.vector.tensor_copy(out, in_).then_inc(done, 1)
-            else:
-                g.scalar.activation(out, in_, copy).then_inc(done, 1)
-
-        gather("v", 0, 0, S, sem["gv%d" % k])
-        gather("v", 1, 0, SPLIT, sem["gv%d" % k])
-        gather("s", 2, 0, S, sem["gs%d" % k])
-        gather("s", 3, 0, S, sem["gs%d" % k])
-        gather("s", 1, SPLIT, S, sem["gs%d" % k])
-        if k == 0:
+            if a == 0:
+                need = len(topo.engines(cores[r], core)[:LIST_ENGINES])
+                g.vector.wait_ge(sem["la%d" % k], need)
+                g.scalar.wait_ge(sem["la%d" % k], need)
+        gv, gs, qd = sem["gv%d" % i], sem["gs%d" % i], sem["q%d" % i]
+        nv = ns = 0
+        for t in range(4):
+            m = a + share[t]
+            out = lambda u, v: w[:, 4 * u + t:4 * v:4]
+            in_ = lambda u, v: T.bd[:, 128 * t:128 * t + 128].indirect(off[:, o0 + u // 16:o0 + v // 16])
+            if m > a:
+                g.vector.tensor_copy(out(a, m), in_(a, m)).then_inc(gv, 1)
+                nv += 1
+            if m < b:
+                g.scalar.activation(out(m, b), in_(m, b), copy).then_inc(gs, 1)
+                ns += 1
+        if i == 0:
             g.vector.wait_ge(sem.x_in, 16)
             g.vector.quantize_mx(T.xq[:], T.xp[:], T.xs[:]).then_inc(sem.x_q, 1)
-        g.vector.wait_ge(sem["gv%d" % k], 2)
-        g.vector.wait_ge(sem["gs%d" % k], 3)
-        g.vector.quantize_mx(T["wq%d" % k][:], T["wp%d" % k][:], w[:]).then_inc(sem["q%d" % k], 1)
+        g.vector.wait_ge(gv, nv)
+        g.vector.wait_ge(gs, ns)
+        g.vector.quantize_mx(T["wq%d" % k][:, a:b], T["wp%d" % k][:, a:b], w[:, 4 * a:4 * b]).then_inc(qd, 1)
+        if roads == "own":
+            continue
+        dst, helper = cores[r], helpers[rank]
+        off_chip, on_chip = topo.engines(core, dst), hop_engines(core, helper, dst, topo)
+        arr, hop = sem["arr%d" % k], sem["hop%d" % i]
+        g.wait_ge(qd, 1)
+        if roads == "both":
+            c = (a + b) // 2
+            g.remote_dma_fused([transfer(helper, codes("aq", k, a, c), codes("wq", k, a, c), hop, on_chip),
+                                transfer(dst, codes("aq", k, c, b), codes("wq", k, c, b), arr, off_chip)], local_sem=sem.sent)
+            sent += len(on_chip) + len(off_chip)
+        elif roads == "helper":
+            sent += send(helper, codes("aq", k, a, b), codes("wq", k, a, b), hop, on_chip)
+        else:
+            sent += send(dst, codes("aq", k, a, b), codes("wq", k, a, b), arr, off_chip)
+        if b == S:
+            sent += send(dst, T["ap%d" % k][:], T["wp%d" % k][:], arr, off_chip)
 
-        if k:
-            dst = cores[r]
-            eng = topo.engines(core, dst)
-            g.wait_ge(sem["q%d" % k], 1)
-            sent += send(dst, T["aq%d" % k][:].bitcast(dt.uint8), T["wq%d" % k][:].bitcast(dt.uint8), sem["arr%d" % k], eng)
-            sent += send(dst, T["ap%d" % k][:], T["wp%d" % k][:], sem["arr%d" % k], eng)
+    def product(k, h, start, stop):
+        s = (rank - k) % N
+        q, p = (T["aq%d" % k], T["ap%d" % k]) if k else (T.wq0, T.wp0)
+        return g.tensor.matmul_mx(T.ps[:, 512 * h:512 * h + H], T.xq[:, 128 * s:128 * s + 128], T.xp[:, 128 * s:128 * s + 128],
+                                  q[:, H * h:H * h + H], p[:, H * h:H * h + H], start, stop)
+
+    def arrived(k):
+        s = (rank - k) % N
+        need = len(topo.engines(cores[s], core))
+        for k2, a, b, share, roads in ORDER:
+            if k2 == k:
+                need += len(topo.engines(helpers[s], core)) if roads in ("helper", "both") else 0
+                need += len(topo.engines(cores[s], core)) if roads in ("direct", "both") else 0
+        g.tensor.wait_ge(sem["arr%d" % k], need)
 
     g.tensor.wait_ge(sem.x_q, 1)
-    for k in range(N):
-        s = (rank - k) % N
-        if k == 0:
-            g.tensor.wait_ge(sem.q0, 1)
-            q, p = T.wq0, T.wp0
-        else:
-            g.tensor.wait_ge(sem["arr%d" % k], 2 * len(topo.engines(cores[s], core)))
-            q, p = T["aq%d" % k], T["ap%d" % k]
-        for h, done in ((0, sem.mm_a), (1, sem.mm_b)):
-            m = g.tensor.matmul_mx(T.ps[:, 512 * h:512 * h + 256], T.xq[:, 128 * s:128 * s + 128], T.xp[:, 128 * s:128 * s + 128],
-                                   q[:, 256 * h:256 * h + 256], p[:, 256 * h:256 * h + 256], k == 0, k == N - 1)
-            if k == N - 1:
-                m.then_inc(done, 1)
+    g.tensor.wait_ge(sem.q0, 1)
+    product(0, 0, True, False)
+    for k in (1, 2):
+        arrived(k)
+        product(k, 0, False, False)
+        product(k, 1, k == 1, False)
+    g.tensor.wait_ge(sem["q%d" % (len(ORDER) - 1)], 1)
+    product(0, 1, False, False)
+    arrived(3)
+    product(3, 0, False, True).then_inc(sem.mm_a, 1)
+    product(3, 1, False, True).then_inc(sem.mm_b, 1)
 
     g.vector.wait_ge(sem.mm_a, 1)
-    g.vector.tensor_copy(T.yo[:, 0:256], T.ps[:, 0:256]).then_inc(sem.y_v, 1)
+    g.vector.tensor_copy(T.yo[:, 0:H], T.ps[:, 0:H]).then_inc(sem.y_v, 1)
     g.sync.wait_ge(sem.y_v, 1)
-    g.sync.dma_start(T.y[:, 0:256], T.yo[:, 0:256]).then_inc(sem.out_a, 16)
+    g.sync.dma_start(T.y[:, 0:H], T.yo[:, 0:H]).then_inc(sem.out_a, 16)
     g.sync.wait_ge(sem.out_a, 16)
     g.scalar.wait_ge(sem.mm_b, 1)
-    g.scalar.activation(T.yo[:, 256:512], T.ps[:, 512:768], copy).then_inc(sem.y_s, 1)
+    g.scalar.activation(T.yo[:, H:S], T.ps[:, 512:512 + H], copy).then_inc(sem.y_s, 1)
     g.scalar.wait_ge(sem.y_s, 1)
-    g.scalar.dma_start(T.y[:, 256:512], T.yo[:, 256:512]).then_inc(sem.out_b, 16)
+    g.scalar.dma_start(T.y[:, H:S], T.yo[:, H:S]).then_inc(sem.out_b, 16)
     g.scalar.wait_ge(sem.out_b, 16)
     g.wait_ge(sem.sent, sent)

from concourse.bass import DstId, RemoteDMATransfer
from concourse.mybir import dt, ActivationFunctionType

N = 4
S = 512
H = S // 2
CODES = "float8_e4m3fn_x4"
LIST_ENGINES = 4
ORDER = [
    (0, 0, H, (256, 160, 0, 0), "own"),
    (1, 0, H, (256, 192, 0, 0), "helper"),
    (1, H, S, (256, 192, 0, 0), "direct"),
    (2, 0, S, (512, 384, 0, 0), "both"),
    (3, 0, H, (256, 192, 0, 0), "helper"),
    (3, H, S, (256, 192, 0, 0), "direct"),
    (0, H, S, (256, 192, 0, 0), "own"),
]

SCRATCH = {
    "cwi": ("sbuf", [128, 128], "int32"),
    "lst": ("sbuf", [128, 128], "uint16"),
    "bks": ("sbuf", [128, 512], "bfloat16"),
    "bd": ("sbuf", [128, 512], "bfloat16"),
    "xs": ("sbuf", [128, 2048], "bfloat16"),
    "xq": ("sbuf", [128, 512], CODES),
    "xp": ("sbuf", [128, 512], "uint8"),
    "yo": ("sbuf", [128, 512], "float32"),
    "ps": ("psum", [128, 1024], "float32"),
}
SEMAPHORES = ["cw_in", "bk_in", "x_in", "lst_v", "bd_v", "bd_s", "x_q", "sent", "mm_a", "mm_b", "y_v", "y_s", "out_a", "out_b"]
for _i in range(len(ORDER)):
    SEMAPHORES += ["gv%d" % _i, "gs%d" % _i, "q%d" % _i, "hop%d" % _i]
for _k in range(N):
    SCRATCH["w%d" % _k] = ("sbuf", [128, 4 * S], "bfloat16")
    SCRATCH["wq%d" % _k] = ("sbuf", [128, S], CODES)
    SCRATCH["wp%d" % _k] = ("sbuf", [128, S], "uint8")
    if _k:
        SCRATCH["la%d" % _k] = ("sbuf", [128, 32], "uint16")
        SCRATCH["aq%d" % _k] = ("sbuf", [128, S], CODES)
        SCRATCH["ap%d" % _k] = ("sbuf", [128, S], "uint8")
        SEMAPHORES += ["la%d" % _k, "arr%d" % _k]


def mask_of(engines):
    return sum(1 << e for e in engines)


def helper_of(core, dsts, topo):
    return [h for h in topo.cores_of(core) if topo.die(h) != topo.die(core) and all(topo.may_write(h, d) for d in dsts)][0]


def hop_engines(src, helper, dst, topo):
    off = topo.engines(src, dst)
    return [e for e in topo.engines(src, helper) if e not in off]


def handed_on(a, b, roads):
    return {"helper": (a, b), "both": (a, (a + b) // 2)}[roads]


def rank_program(g, core, T, topo):
    cores = T.cores
    sem = T.sem
    copy = ActivationFunctionType.Copy

    def codes(name, k, a, b):
        return T["%s%d" % (name, k)][:, a:b].bitcast(dt.uint8)

    def send(dst, out, in_, remote_sem, engines):
        rid, pid, _ = topo.addr(dst)
        g.remote_dma(out, in_, remote_sem, sem.sent, pid, rid, mask_of(engines))
        return len(engines)

    def transfer(dst, out, in_, remote_sem, engines):
        rid, pid, _ = topo.addr(dst)
        return RemoteDMATransfer(dst_ids=[DstId(rid=rid, pnc=pid)], dma_engine_mask=mask_of(engines), remote_sem=remote_sem, src=in_, dst=out)

    helpers = [helper_of(cores[r], [c for c in cores if c != cores[r]], topo) for r in range(N)]
    rank = T.rank_of(core)
    if rank is None:
        if core not in helpers:
            return
        r = helpers.index(core)
        sent = 0
        for i, (k, a, b, share, roads) in enumerate(ORDER):
            if roads in ("helper", "both"):
                a, b = handed_on(a, b, roads)
                dst = cores[(r + k) % N]
                g.wait_ge(sem["hop%d" % i], len(hop_engines(cores[r], core, dst, topo)))
                sent += send(dst, codes("aq", k, a, b), codes("aq", k, a, b), sem["arr%d" % k], topo.engines(core, dst))
        g.wait_ge(sem.sent, sent)
        return

    g.sync.dma_start(T.cwi[:], T.cw[:]).then_inc(sem.cw_in, 16)
    g.scalar.dma_start(T.bks[:], T.bk[:]).then_inc(sem.bk_in, 16)
    g.sync.dma_start(T.xs[:], T.x[:]).then_inc(sem.x_in, 16)

    g.vector.wait_ge(sem.cw_in, 16)
    g.vector.tensor_copy(T.lst[:], T.cwi[:]).then_inc(sem.lst_v, 1)
    g.vector.wait_ge(sem.bk_in, 16)
    for t in (0, 1):
        g.vector.tensor_copy(T.bd[:, 128 * t:128 * t + 128], T.bks[:, t:512:4]).then_inc(sem.bd_v, 1)
    g.scalar.wait_ge(sem.bk_in, 16)
    for t in (2, 3):
        g.scalar.activation(T.bd[:, 128 * t:128 * t + 128], T.bks[:, t:512:4], copy).then_inc(sem.bd_s, 1)
    for q in (g.vector, g.scalar):
        q.wait_ge(sem.bd_v, 2)
        q.wait_ge(sem.bd_s, 2)
        q.wait_ge(sem.lst_v, 1)

    sent = 0
    g.wait_ge(sem.lst_v, 1)
    for k in range(1, N):
        s = (rank - k) % N
        dst = cores[s]
        sent += send(dst, T["la%d" % k][:], T.lst[:, 32 * s:32 * s + 32], sem["la%d" % k], topo.engines(core, dst)[:LIST_ENGINES])

    for i, (k, a, b, share, roads) in enumerate(ORDER):
        r = (rank + k) % N
        w = T["w%d" % k]
        if k == 0:
            off, o0 = T.lst, 32 * rank
        else:
            off, o0 = T["la%d" % k], 0
            if a == 0:
                need = len(topo.engines(cores[r], core)[:LIST_ENGINES])
                g.vector.wait_ge(sem["la%d" % k], need)
                g.scalar.wait_ge(sem["la%d" % k], need)
        gv, gs, qd = sem["gv%d" % i], sem["gs%d" % i], sem["q%d" % i]
        nv = ns = 0
        for t in range(4):
            m = a + share[t]
            out = lambda u, v: w[:, 4 * u + t:4 * v:4]
            in_ = lambda u, v: T.bd[:, 128 * t:128 * t + 128].indirect(off[:, o0 + u // 16:o0 + v // 16])
            if m > a:
                g.vector.tensor_copy(out(a, m), in_(a, m)).then_inc(gv, 1)
                nv += 1
            if m < b:
                g.scalar.activation(out(m, b), in_(m, b), copy).then_inc(gs, 1)
                ns += 1
        if i == 0:
            g.vector.wait_ge(sem.x_in, 16)
            g.vector.quantize_mx(T.xq[:], T.xp[:], T.xs[:]).then_inc(sem.x_q, 1)
        g.vector.wait_ge(gv, nv)
        g.vector.wait_ge(gs, ns)
        g.vector.quantize_mx(T["wq%d" % k][:, a:b], T["wp%d" % k][:, a:b], w[:, 4 * a:4 * b]).then_inc(qd, 1)
        if roads == "own":
            continue
        dst, helper = cores[r], helpers[rank]
        off_chip, on_chip = topo.engines(core, dst), hop_engines(core, helper, dst, topo)
        arr, hop = sem["arr%d" % k], sem["hop%d" % i]
        g.wait_ge(qd, 1)
        if roads == "both":
            c = (a + b) // 2
            g.remote_dma_fused([transfer(helper, codes("aq", k, a, c), codes("wq", k, a, c), hop, on_chip),
                                transfer(dst, codes("aq", k, c, b), codes("wq", k, c, b), arr, off_chip)], local_sem=sem.sent)
            sent += len(on_chip) + len(off_chip)
        elif roads == "helper":
            sent += send(helper, codes("aq", k, a, b), codes("wq", k, a, b), hop, on_chip)
        else:
            sent += send(dst, codes("aq", k, a, b), codes("wq", k, a, b), arr, off_chip)
        if b == S:
            sent += send(dst, T["ap%d" % k][:], T["wp%d" % k][:], arr, off_chip)

    def product(k, h, start, stop):
        s = (rank - k) % N
        q, p = (T["aq%d" % k], T["ap%d" % k]) if k else (T.wq0, T.wp0)
        return g.tensor.matmul_mx(T.ps[:, 512 * h:512 * h + H], T.xq[:, 128 * s:128 * s + 128], T.xp[:, 128 * s:128 * s + 128],
                                  q[:, H * h:H * h + H], p[:, H * h:H * h + H], start, stop)

    def arrived(k):
        s = (rank - k) % N
        need = len(topo.engines(cores[s], core))
        for k2, a, b, share, roads in ORDER:
            if k2 == k:
                need += len(topo.engines(helpers[s], core)) if roads in ("helper", "both") else 0
                need += len(topo.engines(cores[s], core)) if roads in ("direct", "both") else 0
        g.tensor.wait_ge(sem["arr%d" % k], need)

    g.tensor.wait_ge(sem.x_q, 1)
    g.tensor.wait_ge(sem.q0, 1)
    product(0, 0, True, False)
    for k in (1, 2):
        arrived(k)
        product(k, 0, False, False)
        product(k, 1, k == 1, False)
    g.tensor.wait_ge(sem["q%d" % (len(ORDER) - 1)], 1)
    product(0, 1, False, False)
    arrived(3)
    product(3, 0, False, True).then_inc(sem.mm_a, 1)
    product(3, 1, False, True).then_inc(sem.mm_b, 1)

    g.vector.wait_ge(sem.mm_a, 1)
    g.vector.tensor_copy(T.yo[:, 0:H], T.ps[:, 0:H]).then_inc(sem.y_v, 1)
    g.sync.wait_ge(sem.y_v, 1)
    g.sync.dma_start(T.y[:, 0:H], T.yo[:, 0:H]).then_inc(sem.out_a, 16)
    g.sync.wait_ge(sem.out_a, 16)
    g.scalar.wait_ge(sem.mm_b, 1)
    g.scalar.activation(T.yo[:, H:S], T.ps[:, 512:512 + H], copy).then_inc(sem.y_s, 1)
    g.scalar.wait_ge(sem.y_s, 1)
    g.scalar.dma_start(T.y[:, H:S], T.yo[:, H:S]).then_inc(sem.out_b, 16)
    g.scalar.wait_ge(sem.out_b, 16)
    g.wait_ge(sem.sent, sent)
